import numpy as np
import ml_dtypes


def mxq(x, axis, fmt="e4m3"):
    dtype, down = {"e4m3": (ml_dtypes.float8_e4m3fn, 7), "e5m2": (ml_dtypes.float8_e5m2, 14)}[fmt]
    v = np.moveaxis(np.asarray(x, np.float32).astype(ml_dtypes.bfloat16).astype(np.float64), axis, -1)
    blocks = v.reshape(v.shape[:-1] + (-1, 32))
    amax = np.abs(blocks).max(-1, keepdims=True)
    byte = np.maximum(np.where(amax > 0, np.frexp(amax)[1] - 1 + 127, 0) - down, 1)
    scale = np.exp2(byte - 127.0)
    codes = (blocks / scale).astype(np.float32).astype(dtype).astype(np.float64)
    return np.moveaxis((codes * scale).reshape(v.shape), -1, axis)


WIDE = False


def mx_kscale(k):
    if not WIDE:
        return np.ones(k)
    levels = np.array([10, -10, 5, -5, 0])
    if k % 512:
        return np.exp2(np.random.permutation(np.resize(levels, k // 32))).repeat(32)
    a = np.empty((k // 512, 16))
    for p in range(k // 512):
        a[p, :8] = np.random.permutation(np.resize(levels, 8))
        for g in range(8):
            far = levels[np.abs(levels - a[p, g]) >= 10]
            a[p, g + 8] = far[np.random.randint(len(far))]
    return np.exp2(a.ravel()).repeat(32)


def f64(x):
    return np.asarray(x).astype(np.float64)


def striped(idx):
    return np.tile(np.asarray(idx).reshape(-1, 16).T, (8, 1)).astype(np.uint16)


def unstriped(offs):
    return offs[:16].T.reshape(-1).astype(np.int64)


def rot(x):
    y = x.reshape(-1, 2, x.shape[1])
    return np.stack([-y[:, 1], y[:, 0]], axis=1).reshape(x.shape)


def bf(x):
    return np.asarray(x, np.float32).astype(ml_dtypes.bfloat16)


def planes(Y):
    r, m = Y.shape
    b = f64(bf(Y)).reshape(r // 32, 32, m)
    amax = np.abs(b).max(1)
    byte = np.clip(np.where(amax > 0, np.frexp(amax)[1] - 1 + 127 - 7, 1), 1, 254)
    codes = (b * np.exp2(127.0 - byte)[:, None, :]).reshape(r, m).astype(np.float32).astype(ml_dtypes.float8_e4m3fn).view(np.uint8)
    words = codes.reshape(r // 512, 128, 4, m).transpose(0, 1, 3, 2)
    return np.ascontiguousarray(words), np.ascontiguousarray(byte.astype(np.uint8).reshape(r // 512, 16, m))


D, T, I, U, Q = 512, 1024, 512, 1024, 512


def setup_inputs():
    n = np.random.standard_normal
    idx = np.random.permutation(T)[:I]
    idx2 = np.random.permutation(T)[:I]
    idx3 = np.random.randint(0, U, I)
    fd = mx_kscale(D)
    return {
        "query": (n((D, Q)) * 0.8 / np.sqrt(D) * fd[:, None]).astype(np.float32),
        "keys": (n((D, T)) / fd[:, None]).astype(np.float32),
        "cosn": (np.repeat(np.round(np.cos(np.arange(D // 2)[:, None] * 0.11 + np.arange(U)[None] * 0.37) * 64) / 64, 2, axis=0)).astype(np.float32),
        "sinn": (np.repeat(np.round(np.sin(np.arange(D // 2)[:, None] * 0.11 + np.arange(U)[None] * 0.37) * 64) / 64, 2, axis=0)).astype(np.float32),
        "ka": (np.random.uniform(0.4, 0.8, (1, I))).astype(np.float32),
        "kb": (np.random.uniform(0.3, 0.7, (1, I))).astype(np.float32),
        "offs": striped(idx),
        "offs2": striped(idx2),
        "offs3": striped(idx3),
    }


def reference(query, keys, cosn, sinn, ka, kb, offs, offs2, offs3):
    idx = unstriped(offs)
    idx2 = unstriped(offs2)
    idx3 = unstriped(offs3)
    kr = rot(f64(keys)[:, idx2])
    k2 = f64(keys)[:, idx2] * f64(cosn)[:, idx3] + kr * f64(sinn)[:, idx3]
    km = f64(keys)[:, idx] * f64(ka) + k2 * f64(kb)
    queryq = mxq(f64(query), 0, "e4m3")
    kmq = mxq(km, 0, "e4m3")
    a = queryq.T @ kmq
    p = np.exp(a - np.max(a, axis=1, keepdims=True))
    y = p / np.sum(p, axis=1, keepdims=True) * 512.0
    words, scales = planes(y)
    return y, words, scales

@@ -1,0 +1,211 @@
+from contextlib import ExitStack
+
+import concourse.mybir as mybir
+from concourse.masks import make_identity
+
+F32 = mybir.dt.float32
+BF16 = mybir.dt.bfloat16
+I32 = mybir.dt.int32
+U32 = mybir.dt.uint32
+U16 = mybir.dt.uint16
+U8 = mybir.dt.uint8
+FP8X4 = mybir.dt.float8_e4m3fn_x4
+ALU = mybir.AluOpType
+ACT = mybir.ActivationFunctionType
+AXIS = mybir.AxisListType
+
+P = 128
+D, T, SLOTS, Q = 512, 1024, 512, 512
+HALF = SLOTS // 2
+FLOPS = 2 * D * Q * SLOTS
+PIECES = ((0, 256), (256, 128), (384, 128))
+V_COLS = 320
+
+
+def tile_attend_ropemerge_pl_kernel(tc, query, keys, cosn, sinn, ka, kb, offs, offs2, offs3, out_0, out_1, out_2):
+    nc = tc.nc
+    with ExitStack() as ctx:
+        sb = ctx.enter_context(tc.tile_pool(name="sb", bufs=1))
+        ps = ctx.enter_context(tc.psum_pool(name="ps", bufs=1))
+
+        def plane(src, t, name):
+            tile = sb.tile([P, T], F32, name=name)
+            nc.sync.dma_start(tile[:], src.rearrange("(p t) n -> p t n", t=4)[:, t, :])
+            return tile
+
+        def offsets(src, name):
+            tile = sb.tile([P, SLOTS // 16], U16, name=name)
+            nc.sync.dma_start(tile[:], src)
+            return tile
+
+        def share_columns(src, name):
+            tile = sb.tile([P, 4], F32, name=name)
+            nc.scalar.dma_start(tile[:], src.rearrange("o (p s) -> (o p) s", s=4))
+            return tile
+
+        key = [None] * 4
+        cos = [None] * 2
+        sin = [None] * 2
+        key[0] = plane(keys, 0, "key0")
+        list2 = offsets(offs2, "list2")
+        ka_cols = share_columns(ka, "ka_cols")
+        kb_cols = share_columns(kb, "kb_cols")
+        list1 = offsets(offs, "list1")
+        key[1] = plane(keys, 1, "key1")
+        list3 = offsets(offs3, "list3")
+        cos[0] = plane(cosn, 0, "cos0")
+        sin[0] = plane(sinn, 0, "sin0")
+        q_raw = sb.tile([P, 4, Q], F32, name="q_raw")
+        nc.sync.dma_start(q_raw[:], query.rearrange("(p j) q -> p j q", j=4))
+        key[2] = plane(keys, 2, "key2")
+        key[3] = plane(keys, 3, "key3")
+        cos[1] = plane(cosn, 2, "cos1")
+        sin[1] = plane(sinn, 2, "sin1")
+
+        ident = sb.tile([P, P], F32, name="ident")
+        make_identity(nc, ident[:])
+
+        warm = sb.tile([P, 8], F32, name="warm")
+        nc.scalar.activation(warm[:], ident[:, 0:8], ACT.Exp)
+
+        def sum_bank(name):
+            return ps.tile([P, 4, P], F32, name=name, tag="sums", bufs=2)
+
+        def spread(cols, name):
+            bank = sum_bank(name + "_bank")
+            for s in range(4):
+                nc.tensor.transpose(bank[:, s, :], cols[:, s : s + 1].to_broadcast([P, P]), ident[:])
+            row = sb.tile([P, SLOTS], F32, name=name)
+            nc.scalar.copy(row[:].rearrange("j (p s) -> j p s", s=4), bank[:].rearrange("j s p -> j p s"))
+            return row
+
+        ka_row = spread(ka_cols, "ka_row")
+        kb_row = spread(kb_cols, "kb_row")
+
+        def listed(table, offs_tile, lo, n):
+            return table[:].indirect(offs_tile[:, lo // 16 : (lo + n) // 16])
+
+        def first_keys(u):
+            tile = sb.tile([P, 2, SLOTS], F32, name=f"first{u}")
+            for e in range(2):
+                nc.vector.tensor_tensor(tile[:, e, :], listed(key[2 * u + e], list1, 0, SLOTS), ka_row[:], ALU.mult)
+            return tile
+
+        def rotated_terms(u, lo, n):
+            name = f"{u}_{lo}"
+            c = sb.tile([P, n], F32, name="c" + name, tag="c")
+            s = sb.tile([P, n], F32, name="s" + name, tag="s")
+            g = sb.tile([P, 2, n], F32, name="g" + name, tag="g")
+            with_cos = sb.tile([P, 2, n], F32, name="pc" + name)
+            with_sin = sb.tile([P, 2, n], F32, name="ps" + name)
+            nc.vector.tensor_tensor(c[:], listed(cos[u], list3, lo, n), kb_row[:, lo : lo + n], ALU.mult)
+            for e in range(2):
+                nc.vector.tensor_copy(g[:, e, :], listed(key[2 * u + e], list2, lo, n))
+            nc.vector.tensor_tensor(s[:], listed(sin[u], list3, lo, n), kb_row[:, lo : lo + n], ALU.mult)
+            nc.vector.tensor_tensor(with_cos[:], g[:], c[:].unsqueeze(1).to_broadcast([P, 2, n]), ALU.mult)
+            nc.vector.scalar_tensor_tensor(with_sin[:, 0, :], g[:, 1, :], -1.0, s[:], ALU.mult, ALU.mult)
+            nc.vector.tensor_tensor(with_sin[:, 1, :], g[:, 0, :], s[:], ALU.mult)
+            return with_cos, with_sin
+
+        turned = [[None] * 4 for u in range(2)]
+
+        def sum_terms(u, lo, n, terms):
+            bank = sum_bank(f"sum{u}_{lo}")
+            tiles = n // P
+            passes = [(term, base, s, e) for term, base in terms for e in range(2) for s in range(tiles)]
+            for k, (term, base, s, e) in enumerate(passes):
+                at = lo + s * P - base
+                nc.tensor.matmul(
+                    bank[:, 2 * s + e, :], lhsT=term[:, e, at : at + P], rhs=ident[:],
+                    is_transpose=True, start=(k == 0), stop=(k == len(passes) - 1),
+                )
+            tile = sb.tile([P, tiles, P, 2], BF16, name=f"turned{u}_{lo}")
+            nc.scalar.copy(tile[:], bank[:, 0 : 2 * tiles, :].rearrange("i (s e) p -> i s p e", e=2))
+            for s in range(tiles):
+                turned[u][lo // P + s] = tile[:, s, :, :].rearrange("i p e -> i (p e)").bitcast(F32)
+
+        km = [sb.tile([P, HALF, 4], BF16, name=f"km{h}", align_bytes=64) for h in range(2)]
+
+        def turn_back(lo, n):
+            bank = ps.tile([P, 2, n], F32, name=f"back{lo}", tag="back", bufs=2)
+            for u in range(2):
+                for s in range(n // P):
+                    nc.tensor.transpose(bank[:, u, s * P : (s + 1) * P], turned[u][lo // P + s], ident[:])
+            h, at = divmod(lo, HALF)
+            words = km[h][:, at : at + n, :].rearrange("p i t -> p (i t)").bitcast(F32)
+            nc.scalar.copy(words.rearrange("p (i u) -> p i u", u=2), bank[:].rearrange("p u i -> p i u"))
+
+        first = first_keys(0)
+        with_cos, with_sin = rotated_terms(0, 0, SLOTS)
+        for lo in (0, HALF):
+            sum_terms(0, lo, HALF, ((first, 0), (with_cos, 0), (with_sin, 0)))
+
+        q_bf = sb.tile([P, 4, P, 4], BF16, name="q_bf", align_bytes=64)
+        for t in range(4):
+            nc.scalar.copy(q_bf[:, t, :, :], q_raw[:].rearrange("p j (m t) -> p t m j", t=4)[:, t, :, :])
+        q_codes = sb.tile([P, Q], U32, name="q_codes", align_bytes=64)
+        q_scales = sb.tile([P, Q], U8, name="q_scales", align_bytes=64)
+        nc.vector.quantize_mx(out=q_codes[:].bitcast(FP8X4), scales=q_scales[:], in_=q_bf[:].rearrange("p t m j -> p (t m j)"))
+
+        scores = [ps.tile([P, SLOTS], F32, name=f"scores{t}") for t in range(4)]
+
+        def score(h):
+            codes = sb.tile([P, HALF], U32, name=f"k_codes{h}", align_bytes=64)
+            scales = sb.tile([P, HALF], U8, name=f"k_scales{h}", align_bytes=64)
+            nc.vector.quantize_mx(out=codes[:].bitcast(FP8X4), scales=scales[:], in_=km[h][:].rearrange("p i t -> p (i t)"))
+            for t in range(4):
+                rows = slice(t * P, (t + 1) * P)
+                nc.tensor.matmul_mx(
+                    out=scores[t][:, h * HALF : (h + 1) * HALF],
+                    lhsT=q_codes[:, rows].bitcast(FP8X4), lhsT_scale=q_scales[:, rows],
+                    rhs=codes[:].bitcast(FP8X4), rhs_scale=scales[:], start=True, stop=True,
+                )
+
+        neg_max_half = sb.tile([P, 4], F32, name="neg_max_half")
+        first = first_keys(1)
+        for lo, n in PIECES:
+            with_cos, with_sin = rotated_terms(1, lo, n)
+            sum_terms(1, lo, n, ((first, 0), (with_cos, lo), (with_sin, lo)))
+            turn_back(lo, n)
+            if lo + n == HALF:
+                score(0)
+        for t in range(4):
+            nc.vector.tensor_reduce(neg_max_half[:, t : t + 1], scores[t][:, 0:HALF], AXIS.X, ALU.max, negate=True)
+        score(1)
+
+        neg_max = sb.tile([P, 4], F32, name="neg_max")
+        sums = sb.tile([P, 4], F32, name="sums")
+        inv = sb.tile([P, 4], F32, name="inv")
+        negated = sb.tile([P, HALF], F32, name="negated")
+        p = sb.tile([P, 4, SLOTS], F32, name="p")
+        y = sb.tile([P, 4, SLOTS], F32, name="y")
+        out_rows = out_0.rearrange("(p t) i -> p t i", t=4)
+        for t in range(4):
+            col = slice(t, t + 1)
+            nc.vector.tensor_scalar(
+                negated[:], scores[t][:, HALF:SLOTS], -1.0, neg_max_half[:, col], ALU.mult, ALU.min, accum_out=neg_max[:, col]
+            )
+            nc.scalar.activation(p[:, t, :], scores[t][:], ACT.Exp, bias=neg_max[:, col], accum_out=sums[:, col])
+        for t in range(4):
+            col = slice(t, t + 1)
+            nc.vector.reciprocal(inv[:, col], sums[:, col])
+            nc.vector.tensor_scalar(y[:, t, :], p[:, t, :], inv[:, col], 512.0, ALU.mult, ALU.mult)
+            nc.sync.dma_start(out_rows[:, t, :], y[:, t, :])
+
+        y_bf = sb.tile([P, SLOTS, 4], BF16, name="y_bf", align_bytes=64)
+
+        def woven(cols):
+            return (
+                y_bf[:, cols, :].rearrange("p (c i) t -> p c t i", i=4),
+                y[:, :, cols].rearrange("p t (c i) -> p c t i", i=4),
+            )
+
+        nc.vector.tensor_copy(*woven(slice(0, V_COLS)))
+        nc.scalar.copy(*woven(slice(V_COLS, SLOTS)))
+        y_codes = sb.tile([P, SLOTS], U32, name="y_codes", align_bytes=64)
+        y_scales = sb.tile([P, SLOTS], U8, name="y_scales", align_bytes=64)
+        nc.vector.quantize_mx(out=y_codes[:].bitcast(FP8X4), scales=y_scales[:], in_=y_bf[:].rearrange("p c t -> p (c t)"))
+        nc.sync.dma_start(out_1[0].rearrange("p c r -> p (c r)").bitcast(I32), y_codes[:].bitcast(I32))
+        for quad in range(4):
+            queue = nc.scalar if quad < 2 else nc.sync
+            queue.dma_start(out_2[0, 4 * quad : 4 * quad + 4, :].bitcast(I32), y_scales[32 * quad : 32 * quad + 4, :].bitcast(I32))

@@ -20,6 +20,9 @@ HALF = SLOTS // 2
 FLOPS = 2 * D * Q * SLOTS
 PIECES = ((0, 256), (256, 128), (384, 128))
 V_COLS = 320
+LOADS = "k0 l2 l1 k1 l3 q c0 s0 k2 k3 c1 s1".split()
+GB, CB, SB = 2, 1, 1
+SPLIT_PC = False
 
 
 def tile_attend_ropemerge_pl_kernel(tc, query, keys, cosn, sinn, ka, kb, offs, offs2, offs3, out_0, out_1, out_2):
@@ -38,29 +41,29 @@ def tile_attend_ropemerge_pl_kernel(tc, query, keys, cosn, sinn, ka, kb, offs, o
             nc.sync.dma_start(tile[:], src)
             return tile
 
-        def share_columns(src, name):
-            tile = sb.tile([P, 4], F32, name=name)
-            nc.scalar.dma_start(tile[:], src.rearrange("o (p s) -> (o p) s", s=4))
-            return tile
-
         key = [None] * 4
         cos = [None] * 2
         sin = [None] * 2
-        key[0] = plane(keys, 0, "key0")
-        list2 = offsets(offs2, "list2")
-        ka_cols = share_columns(ka, "ka_cols")
-        kb_cols = share_columns(kb, "kb_cols")
-        list1 = offsets(offs, "list1")
-        key[1] = plane(keys, 1, "key1")
-        list3 = offsets(offs3, "list3")
-        cos[0] = plane(cosn, 0, "cos0")
-        sin[0] = plane(sinn, 0, "sin0")
+        share_rows = sb.tile([P, P], F32, name="share_rows")
+        nc.gpsimd.memset(share_rows[:], 0.0)
+        nc.scalar.dma_start(share_rows[0:4, :], ka.rearrange("o (s i) -> (o s) i", s=4))
+        nc.scalar.dma_start(share_rows[4:8, :], kb.rearrange("o (s i) -> (o s) i", s=4))
         q_raw = sb.tile([P, 4, Q], F32, name="q_raw")
-        nc.sync.dma_start(q_raw[:], query.rearrange("(p j) q -> p j q", j=4))
-        key[2] = plane(keys, 2, "key2")
-        key[3] = plane(keys, 3, "key3")
-        cos[1] = plane(cosn, 2, "cos1")
-        sin[1] = plane(sinn, 2, "sin1")
+        for item in LOADS:
+            if item[0] == "k":
+                key[int(item[1])] = plane(keys, int(item[1]), "key" + item[1])
+            elif item[0] == "c":
+                cos[int(item[1])] = plane(cosn, 2 * int(item[1]), "cos" + item[1])
+            elif item[0] == "s":
+                sin[int(item[1])] = plane(sinn, 2 * int(item[1]), "sin" + item[1])
+            elif item == "q":
+                nc.sync.dma_start(q_raw[:], query.rearrange("(p j) q -> p j q", j=4))
+            elif item == "l1":
+                list1 = offsets(offs, "list1")
+            elif item == "l2":
+                list2 = offsets(offs2, "list2")
+            else:
+                list3 = offsets(offs3, "list3")
 
         ident = sb.tile([P, P], F32, name="ident")
         make_identity(nc, ident[:])
@@ -68,19 +71,13 @@ def tile_attend_ropemerge_pl_kernel(tc, query, keys, cosn, sinn, ka, kb, offs, o
         warm = sb.tile([P, 8], F32, name="warm")
         nc.scalar.activation(warm[:], ident[:, 0:8], ACT.Exp)
 
-        def sum_bank(name):
-            return ps.tile([P, 4, P], F32, name=name, tag="sums", bufs=2)
+        def ring_bank(name):
+            return ps.tile([P, 4, P], F32, name=name, tag="ring", bufs=2)
 
-        def spread(cols, name):
-            bank = sum_bank(name + "_bank")
-            for s in range(4):
-                nc.tensor.transpose(bank[:, s, :], cols[:, s : s + 1].to_broadcast([P, P]), ident[:])
-            row = sb.tile([P, SLOTS], F32, name=name)
-            nc.scalar.copy(row[:].rearrange("j (p s) -> j p s", s=4), bank[:].rearrange("j s p -> j p s"))
-            return row
-
-        ka_row = spread(ka_cols, "ka_row")
-        kb_row = spread(kb_cols, "kb_row")
+        bank = ring_bank("share_bank")
+        nc.tensor.transpose(bank[:, 0, :], share_rows[:], ident[:])
+        shares = sb.tile([P, 8], F32, name="shares")
+        nc.scalar.copy(shares[:], bank[:, 0, 0:8])
 
         def listed(table, offs_tile, lo, n):
             return table[:].indirect(offs_tile[:, lo // 16 : (lo + n) // 16])
@@ -88,66 +85,84 @@ def tile_attend_ropemerge_pl_kernel(tc, query, keys, cosn, sinn, ka, kb, offs, o
         def first_keys(u):
             tile = sb.tile([P, 2, SLOTS], F32, name=f"first{u}")
             for e in range(2):
-                nc.vector.tensor_tensor(tile[:, e, :], listed(key[2 * u + e], list1, 0, SLOTS), ka_row[:], ALU.mult)
+                nc.vector.tensor_copy(tile[:, e, :], listed(key[2 * u + e], list1, 0, SLOTS))
             return tile
 
         def rotated_terms(u, lo, n):
             name = f"{u}_{lo}"
-            c = sb.tile([P, n], F32, name="c" + name, tag="c")
-            s = sb.tile([P, n], F32, name="s" + name, tag="s")
-            g = sb.tile([P, 2, n], F32, name="g" + name, tag="g")
+            c = sb.tile([P, n], F32, name="c" + name, tag="c", bufs=CB)
+            s = sb.tile([P, n], F32, name="s" + name, tag="sq" if (u, lo) == (1, 0) else "s", align_bytes=64, bufs=1 if (u, lo) == (1, 0) else SB)
+            g = sb.tile([P, 2, n], F32, name="g" + name, tag="g", bufs=GB)
             with_cos = sb.tile([P, 2, n], F32, name="pc" + name)
             with_sin = sb.tile([P, 2, n], F32, name="ps" + name)
-            nc.vector.tensor_tensor(c[:], listed(cos[u], list3, lo, n), kb_row[:, lo : lo + n], ALU.mult)
+            nc.vector.tensor_copy(c[:], listed(cos[u], list3, lo, n))
             for e in range(2):
                 nc.vector.tensor_copy(g[:, e, :], listed(key[2 * u + e], list2, lo, n))
-            nc.vector.tensor_tensor(s[:], listed(sin[u], list3, lo, n), kb_row[:, lo : lo + n], ALU.mult)
-            nc.vector.tensor_tensor(with_cos[:], g[:], c[:].unsqueeze(1).to_broadcast([P, 2, n]), ALU.mult)
+            nc.vector.tensor_copy(s[:], listed(sin[u], list3, lo, n))
+            if SPLIT_PC:
+                for e in range(2):
+                    nc.vector.tensor_tensor(with_cos[:, e, :], g[:, e, :], c[:], ALU.mult)
+            else:
+                nc.vector.tensor_tensor(with_cos[:], g[:], c[:].unsqueeze(1).to_broadcast([P, 2, n]), ALU.mult)
             nc.vector.scalar_tensor_tensor(with_sin[:, 0, :], g[:, 1, :], -1.0, s[:], ALU.mult, ALU.mult)
             nc.vector.tensor_tensor(with_sin[:, 1, :], g[:, 0, :], s[:], ALU.mult)
             return with_cos, with_sin
 
-        turned = [[None] * 4 for u in range(2)]
+        merged = [ps.tile([P, 4, P], F32, name=f"merged{s}", tag=f"merged{s}") for s in range(4)]
 
-        def sum_terms(u, lo, n, terms):
-            bank = sum_bank(f"sum{u}_{lo}")
+        def add_share(u, lo, n, terms, base, second):
+            name = f"{u}_{lo}_{second}"
+            if u == 1 and second == 1:
+                bank = ps.tile([P, 4, P], F32, name="turned" + name, tag="last", bufs=2)
+            else:
+                bank = ring_bank("turned" + name)
             tiles = n // P
-            passes = [(term, base, s, e) for term, base in terms for e in range(2) for s in range(tiles)]
-            for k, (term, base, s, e) in enumerate(passes):
+            passes = [(term, s, e) for term in terms for e in range(2) for s in range(tiles)]
+            for k, (term, s, e) in enumerate(passes):
                 at = lo + s * P - base
                 nc.tensor.matmul(
                     bank[:, 2 * s + e, :], lhsT=term[:, e, at : at + P], rhs=ident[:],
                     is_transpose=True, start=(k == 0), stop=(k == len(passes) - 1),
                 )
-            tile = sb.tile([P, tiles, P, 2], BF16, name=f"turned{u}_{lo}")
-            nc.scalar.copy(tile[:], bank[:, 0 : 2 * tiles, :].rearrange("i (s e) p -> i s p e", e=2))
             for s in range(tiles):
-                turned[u][lo // P + s] = tile[:, s, :, :].rearrange("i p e -> i (p e)").bitcast(F32)
+                tile_no = lo // P + s
+                col = 4 * second + tile_no
+                scaled = sb.tile([P, 2, P], F32, name=f"scaled{name}_{s}")
+                nc.scalar.activation(scaled[:], bank[:, 2 * s : 2 * s + 2, :], ACT.Copy, scale=shares[:, col : col + 1])
+                for e in range(2):
+                    nc.tensor.matmul(
+                        merged[tile_no][:, 2 * u + e, :], lhsT=scaled[:, e, :], rhs=ident[:], is_transpose=True,
+                        start=(u == 0 and second == 0 and e == 0), stop=(u == 1 and second == 1 and e == 1),
+                    )
 
         km = [sb.tile([P, HALF, 4], BF16, name=f"km{h}", align_bytes=64) for h in range(2)]
 
-        def turn_back(lo, n):
-            bank = ps.tile([P, 2, n], F32, name=f"back{lo}", tag="back", bufs=2)
-            for u in range(2):
-                for s in range(n // P):
-                    nc.tensor.transpose(bank[:, u, s * P : (s + 1) * P], turned[u][lo // P + s], ident[:])
-            h, at = divmod(lo, HALF)
-            words = km[h][:, at : at + n, :].rearrange("p i t -> p (i t)").bitcast(F32)
-            nc.scalar.copy(words.rearrange("p (i u) -> p i u", u=2), bank[:].rearrange("p u i -> p i u"))
+        def round_merged(lo, n):
+            for s in range(lo // P, (lo + n) // P):
+                h, at = divmod(s * P, HALF)
+                nc.scalar.copy(km[h][:, at : at + P, :], merged[s][:].rearrange("p t i -> p i t"))
 
         first = first_keys(0)
+        for lo in (0, HALF):
+            add_share(0, lo, HALF, (first,), 0, 0)
         with_cos, with_sin = rotated_terms(0, 0, SLOTS)
         for lo in (0, HALF):
-            sum_terms(0, lo, HALF, ((first, 0), (with_cos, 0), (with_sin, 0)))
+            add_share(0, lo, HALF, (with_cos, with_sin), 0, 1)
 
         q_bf = sb.tile([P, 4, P, 4], BF16, name="q_bf", align_bytes=64)
-        for t in range(4):
-            nc.scalar.copy(q_bf[:, t, :, :], q_raw[:].rearrange("p j (m t) -> p t m j", t=4)[:, t, :, :])
+        for m in range(0, P, 32):
+            nc.scalar.copy(
+                q_bf[:].rearrange("p t m j -> p m j t")[:, m : m + 32, :, :],
+                q_raw[:].rearrange("p j (m t) -> p m j t", t=4)[:, m : m + 32, :, :],
+            )
         q_codes = sb.tile([P, Q], U32, name="q_codes", align_bytes=64)
-        q_scales = sb.tile([P, Q], U8, name="q_scales", align_bytes=64)
-        nc.vector.quantize_mx(out=q_codes[:].bitcast(FP8X4), scales=q_scales[:], in_=q_bf[:].rearrange("p t m j -> p (t m j)"))
 
-        scores = [ps.tile([P, SLOTS], F32, name=f"scores{t}") for t in range(4)]
+        scores = []
+        held = []
+
+        def q_scales_tile():
+            held.append(sb.tile([P, Q], U8, name="q_scales", tag="sq", align_bytes=64))
+            return held[0]
 
         def score(h):
             codes = sb.tile([P, HALF], U32, name=f"k_codes{h}", align_bytes=64)
@@ -157,17 +172,25 @@ def tile_attend_ropemerge_pl_kernel(tc, query, keys, cosn, sinn, ka, kb, offs, o
                 rows = slice(t * P, (t + 1) * P)
                 nc.tensor.matmul_mx(
                     out=scores[t][:, h * HALF : (h + 1) * HALF],
-                    lhsT=q_codes[:, rows].bitcast(FP8X4), lhsT_scale=q_scales[:, rows],
+                    lhsT=q_codes[:, rows].bitcast(FP8X4), lhsT_scale=held[0][:, rows],
                     rhs=codes[:].bitcast(FP8X4), rhs_scale=scales[:], start=True, stop=True,
                 )
 
         neg_max_half = sb.tile([P, 4], F32, name="neg_max_half")
         first = first_keys(1)
+        for lo in (0, HALF):
+            add_share(1, lo, HALF, (first,), 0, 0)
         for lo, n in PIECES:
-            with_cos, with_sin = rotated_terms(1, lo, n)
-            sum_terms(1, lo, n, ((first, 0), (with_cos, lo), (with_sin, lo)))
-            turn_back(lo, n)
-            if lo + n == HALF:
+            terms = rotated_terms(1, lo, n)
+            for at in range(lo, lo + n, HALF):
+                add_share(1, at, min(HALF, lo + n - at), terms, lo, 1)
+                round_merged(at, min(HALF, lo + n - at))
+            if lo == 0:
+                nc.vector.quantize_mx(out=q_codes[:].bitcast(FP8X4), scales=q_scales_tile()[:], in_=q_bf[:].rearrange("p t m j -> p (t m j)"))
+                for t in range(2):
+                    scores.append(ring_bank(f"scores{t}")[:].rearrange("p s i -> p (s i)"))
+                for t in range(2):
+                    scores.append(ps.tile([P, SLOTS], F32, name=f"scores{t + 2}", tag=f"merged{t}")[:])
                 score(0)
         for t in range(4):
             nc.vector.tensor_reduce(neg_max_half[:, t : t + 1], scores[t][:, 0:HALF], AXIS.X, ALU.max, negate=True)

@@ -18,11 +18,9 @@ P = 128
 D, T, SLOTS, Q = 512, 1024, 512, 512
 HALF = SLOTS // 2
 FLOPS = 2 * D * Q * SLOTS
-PIECES = ((0, 256), (256, 128), (384, 128))
 V_COLS = 320
-LOADS = "k0 l2 l1 k1 l3 q c0 s0 k2 k3 c1 s1".split()
-GB, CB, SB = 2, 1, 1
-SPLIT_PC = False
+LOADS = "c0 l3 k0 l2 l1 k1 s0 q c1 k2 k3 s1".split()
+POOL_Y = 0
 
 
 def tile_attend_ropemerge_pl_kernel(tc, query, keys, cosn, sinn, ka, kb, offs, offs2, offs3, out_0, out_1, out_2):
@@ -32,7 +30,7 @@ def tile_attend_ropemerge_pl_kernel(tc, query, keys, cosn, sinn, ka, kb, offs, o
         ps = ctx.enter_context(tc.psum_pool(name="ps", bufs=1))
 
         def plane(src, t, name):
-            tile = sb.tile([P, T], F32, name=name)
+            tile = sb.tile([P, T], F32, name=name, tag=name)
             nc.sync.dma_start(tile[:], src.rearrange("(p t) n -> p t n", t=4)[:, t, :])
             return tile
 
@@ -72,59 +70,44 @@ def tile_attend_ropemerge_pl_kernel(tc, query, keys, cosn, sinn, ka, kb, offs, o
         nc.scalar.activation(warm[:], ident[:, 0:8], ACT.Exp)
 
         def ring_bank(name):
-            return ps.tile([P, 4, P], F32, name=name, tag="ring", bufs=2)
+            return ps.tile([P, 4, P], F32, name=name, tag="ring", bufs=4)
 
         bank = ring_bank("share_bank")
         nc.tensor.transpose(bank[:, 0, :], share_rows[:], ident[:])
         shares = sb.tile([P, 8], F32, name="shares")
         nc.scalar.copy(shares[:], bank[:, 0, 0:8])
+        bank = ring_bank("ka_bank")
+        for s in range(4):
+            nc.tensor.transpose(bank[:, s, :], shares[:, s : s + 1].to_broadcast([P, P]), ident[:])
+        ka_row = sb.tile([P, SLOTS], F32, name="ka_row")
+        nc.scalar.copy(ka_row[:], bank[:].rearrange("j s i -> j (s i)"))
 
-        def listed(table, offs_tile, lo, n):
-            return table[:].indirect(offs_tile[:, lo // 16 : (lo + n) // 16])
-
-        def first_keys(u):
-            tile = sb.tile([P, 2, SLOTS], F32, name=f"first{u}")
-            for e in range(2):
-                nc.vector.tensor_copy(tile[:, e, :], listed(key[2 * u + e], list1, 0, SLOTS))
+        def gathered(table, offs_tile, name, align=None):
+            tile = sb.tile([P, SLOTS], F32, name=name, tag=name, align_bytes=64)
+            nc.vector.tensor_copy(tile[:], table[:].indirect(offs_tile[:]))
             return tile
 
-        def rotated_terms(u, lo, n):
-            name = f"{u}_{lo}"
-            c = sb.tile([P, n], F32, name="c" + name, tag="c", bufs=CB)
-            s = sb.tile([P, n], F32, name="s" + name, tag="sq" if (u, lo) == (1, 0) else "s", align_bytes=64, bufs=1 if (u, lo) == (1, 0) else SB)
-            g = sb.tile([P, 2, n], F32, name="g" + name, tag="g", bufs=GB)
-            with_cos = sb.tile([P, 2, n], F32, name="pc" + name)
-            with_sin = sb.tile([P, 2, n], F32, name="ps" + name)
-            nc.vector.tensor_copy(c[:], listed(cos[u], list3, lo, n))
+        def second_keys(u):
+            c = gathered(cos[u], list3, f"c{u}")
+            g = [gathered(key[2 * u + e], list2, f"g{u}{e}") for e in range(2)]
+            with_cos = sb.tile([P, 2, SLOTS], F32, name=f"pc{u}")
             for e in range(2):
-                nc.vector.tensor_copy(g[:, e, :], listed(key[2 * u + e], list2, lo, n))
-            nc.vector.tensor_copy(s[:], listed(sin[u], list3, lo, n))
-            if SPLIT_PC:
-                for e in range(2):
-                    nc.vector.tensor_tensor(with_cos[:, e, :], g[:, e, :], c[:], ALU.mult)
-            else:
-                nc.vector.tensor_tensor(with_cos[:], g[:], c[:].unsqueeze(1).to_broadcast([P, 2, n]), ALU.mult)
-            nc.vector.scalar_tensor_tensor(with_sin[:, 0, :], g[:, 1, :], -1.0, s[:], ALU.mult, ALU.mult)
-            nc.vector.tensor_tensor(with_sin[:, 1, :], g[:, 0, :], s[:], ALU.mult)
-            return with_cos, with_sin
+                nc.gpsimd.tensor_tensor(with_cos[:, e, :], g[e][:], c[:], ALU.mult)
+            return g, with_cos
 
-        merged = [ps.tile([P, 4, P], F32, name=f"merged{s}", tag=f"merged{s}") for s in range(4)]
+        merged = [ps.tile([P, 4, P], F32, name=f"merged{s}") for s in range(4)]
 
-        def add_share(u, lo, n, terms, base, second):
+        def add_share(u, lo, terms, second, opens, closes):
             name = f"{u}_{lo}_{second}"
-            if u == 1 and second == 1:
-                bank = ps.tile([P, 4, P], F32, name="turned" + name, tag="last", bufs=2)
-            else:
-                bank = ring_bank("turned" + name)
-            tiles = n // P
-            passes = [(term, s, e) for term in terms for e in range(2) for s in range(tiles)]
+            bank = ring_bank("turned" + name)
+            passes = [(term, s, e) for term in terms for e in range(2) for s in range(2)]
             for k, (term, s, e) in enumerate(passes):
-                at = lo + s * P - base
+                at = lo + s * P
                 nc.tensor.matmul(
                     bank[:, 2 * s + e, :], lhsT=term[:, e, at : at + P], rhs=ident[:],
                     is_transpose=True, start=(k == 0), stop=(k == len(passes) - 1),
                 )
-            for s in range(tiles):
+            for s in range(2):
                 tile_no = lo // P + s
                 col = 4 * second + tile_no
                 scaled = sb.tile([P, 2, P], F32, name=f"scaled{name}_{s}")
@@ -132,87 +115,80 @@ def tile_attend_ropemerge_pl_kernel(tc, query, keys, cosn, sinn, ka, kb, offs, o
                 for e in range(2):
                     nc.tensor.matmul(
                         merged[tile_no][:, 2 * u + e, :], lhsT=scaled[:, e, :], rhs=ident[:], is_transpose=True,
-                        start=(u == 0 and second == 0 and e == 0), stop=(u == 1 and second == 1 and e == 1),
+                        start=(opens and e == 0), stop=(closes and e == 1),
                     )
 
-        km = [sb.tile([P, HALF, 4], BF16, name=f"km{h}", align_bytes=64) for h in range(2)]
+        km = sb.tile([P, SLOTS, 4], BF16, name="km", align_bytes=64)
 
-        def round_merged(lo, n):
-            for s in range(lo // P, (lo + n) // P):
-                h, at = divmod(s * P, HALF)
-                nc.scalar.copy(km[h][:, at : at + P, :], merged[s][:].rearrange("p t i -> p i t"))
-
-        first = first_keys(0)
+        g, with_cos = second_keys(0)
+        first = sb.tile([P, 2, SLOTS], F32, name="first0")
+        for e in range(2):
+            nc.vector.tensor_copy(first[:, e, :], key[e][:].indirect(list1[:]))
+        s0 = gathered(sin[0], list3, "s0")
+        minus_s0 = sb.tile([P, SLOTS], F32, name="minus_s0")
+        nc.scalar.mul(minus_s0[:], s0[:], -1.0)
+        with_sin = sb.tile([P, 2, SLOTS], F32, name="ps0")
+        nc.gpsimd.tensor_tensor(with_sin[:, 1, :], g[0][:], s0[:], ALU.mult)
+        nc.gpsimd.tensor_tensor(with_sin[:, 0, :], g[1][:], minus_s0[:], ALU.mult)
         for lo in (0, HALF):
-            add_share(0, lo, HALF, (first,), 0, 0)
-        with_cos, with_sin = rotated_terms(0, 0, SLOTS)
-        for lo in (0, HALF):
-            add_share(0, lo, HALF, (with_cos, with_sin), 0, 1)
-
+            add_share(0, lo, (first,), 0, True, False)
         q_bf = sb.tile([P, 4, P, 4], BF16, name="q_bf", align_bytes=64)
         for m in range(0, P, 32):
             nc.scalar.copy(
                 q_bf[:].rearrange("p t m j -> p m j t")[:, m : m + 32, :, :],
                 q_raw[:].rearrange("p j (m t) -> p m j t", t=4)[:, m : m + 32, :, :],
             )
-        q_codes = sb.tile([P, Q], U32, name="q_codes", align_bytes=64)
-
-        scores = []
-        held = []
-
-        def q_scales_tile():
-            held.append(sb.tile([P, Q], U8, name="q_scales", tag="sq", align_bytes=64))
-            return held[0]
-
-        def score(h):
-            codes = sb.tile([P, HALF], U32, name=f"k_codes{h}", align_bytes=64)
-            scales = sb.tile([P, HALF], U8, name=f"k_scales{h}", align_bytes=64)
-            nc.vector.quantize_mx(out=codes[:].bitcast(FP8X4), scales=scales[:], in_=km[h][:].rearrange("p i t -> p (i t)"))
-            for t in range(4):
-                rows = slice(t * P, (t + 1) * P)
-                nc.tensor.matmul_mx(
-                    out=scores[t][:, h * HALF : (h + 1) * HALF],
-                    lhsT=q_codes[:, rows].bitcast(FP8X4), lhsT_scale=held[0][:, rows],
-                    rhs=codes[:].bitcast(FP8X4), rhs_scale=scales[:], start=True, stop=True,
-                )
-
-        neg_max_half = sb.tile([P, 4], F32, name="neg_max_half")
-        first = first_keys(1)
         for lo in (0, HALF):
-            add_share(1, lo, HALF, (first,), 0, 0)
-        for lo, n in PIECES:
-            terms = rotated_terms(1, lo, n)
-            for at in range(lo, lo + n, HALF):
-                add_share(1, at, min(HALF, lo + n - at), terms, lo, 1)
-                round_merged(at, min(HALF, lo + n - at))
-            if lo == 0:
-                nc.vector.quantize_mx(out=q_codes[:].bitcast(FP8X4), scales=q_scales_tile()[:], in_=q_bf[:].rearrange("p t m j -> p (t m j)"))
-                for t in range(2):
-                    scores.append(ring_bank(f"scores{t}")[:].rearrange("p s i -> p (s i)"))
-                for t in range(2):
-                    scores.append(ps.tile([P, SLOTS], F32, name=f"scores{t + 2}", tag=f"merged{t}")[:])
-                score(0)
-        for t in range(4):
-            nc.vector.tensor_reduce(neg_max_half[:, t : t + 1], scores[t][:, 0:HALF], AXIS.X, ALU.max, negate=True)
-        score(1)
+            add_share(0, lo, (with_cos, with_sin), 1, False, True)
+        for s in range(4):
+            nc.scalar.copy(km[:, s * P : (s + 1) * P, 0:2], merged[s][:, 0:2, :].rearrange("p e i -> p i e"))
+
+        g, with_cos = second_keys(1)
+        s1 = gathered(sin[1], list3, "s1")
+        with_sin = sb.tile([P, 2, SLOTS], F32, name="ps1")
+        for lo in (0, HALF):
+            cols = slice(lo, lo + HALF)
+            nc.vector.tensor_tensor(with_sin[:, 1, cols], g[0][:, cols], s1[:, cols], ALU.mult)
+            nc.vector.scalar_tensor_tensor(with_sin[:, 0, cols], g[1][:, cols], -1.0, s1[:, cols], ALU.mult, ALU.mult)
+            add_share(1, lo, (with_cos, with_sin), 1, True, True)
+        first = sb.tile([P, 2, SLOTS], F32, name="first1", tag="sin1")
+        for e in range(2):
+            nc.vector.tensor_tensor(first[:, e, :], key[2 + e][:].indirect(list1[:]), ka_row[:], ALU.mult)
+
+        q_codes = sb.tile([P, Q], U32, name="q_codes", align_bytes=64)
+        q_scales = sb.tile([P, Q], U8, name="q_scales", tag="s1", align_bytes=64)
+        nc.vector.quantize_mx(out=q_codes[:].bitcast(FP8X4), scales=q_scales[:], in_=q_bf[:].rearrange("p t m j -> p (t m j)"))
+
+        for s in range(4):
+            cols = slice(s * P, (s + 1) * P)
+            nc.vector.tensor_tensor(
+                km[:, cols, 2:4], merged[s][:, 2:4, :].rearrange("p e i -> p i e"), first[:, :, cols].rearrange("p e i -> p i e"), ALU.add
+            )
+        k_codes = sb.tile([P, SLOTS], U32, name="k_codes", align_bytes=64)
+        k_scales = sb.tile([P, SLOTS], U8, name="k_scales", align_bytes=64)
+        nc.vector.quantize_mx(out=k_codes[:].bitcast(FP8X4), scales=k_scales[:], in_=km[:].rearrange("p i t -> p (i t)"))
 
         neg_max = sb.tile([P, 4], F32, name="neg_max")
         sums = sb.tile([P, 4], F32, name="sums")
         inv = sb.tile([P, 4], F32, name="inv")
-        negated = sb.tile([P, HALF], F32, name="negated")
         p = sb.tile([P, 4, SLOTS], F32, name="p")
         y = sb.tile([P, 4, SLOTS], F32, name="y")
         out_rows = out_0.rearrange("(p t) i -> p t i", t=4)
         for t in range(4):
             col = slice(t, t + 1)
-            nc.vector.tensor_scalar(
-                negated[:], scores[t][:, HALF:SLOTS], -1.0, neg_max_half[:, col], ALU.mult, ALU.min, accum_out=neg_max[:, col]
+            rows = slice(t * P, (t + 1) * P)
+            scores = ring_bank(f"scores{t}")[:].rearrange("p s i -> p (s i)")
+            nc.tensor.matmul_mx(
+                out=scores, lhsT=q_codes[:, rows].bitcast(FP8X4), lhsT_scale=q_scales[:, rows],
+                rhs=k_codes[:].bitcast(FP8X4), rhs_scale=k_scales[:], start=True, stop=True,
             )
-            nc.scalar.activation(p[:, t, :], scores[t][:], ACT.Exp, bias=neg_max[:, col], accum_out=sums[:, col])
+            nc.vector.tensor_reduce(neg_max[:, col], scores, AXIS.X, ALU.max, negate=True)
+            nc.scalar.activation(p[:, t, :], scores, ACT.Exp, bias=neg_max[:, col], accum_out=sums[:, col])
         for t in range(4):
             col = slice(t, t + 1)
             nc.vector.reciprocal(inv[:, col], sums[:, col])
-            nc.vector.tensor_scalar(y[:, t, :], p[:, t, :], inv[:, col], 512.0, ALU.mult, ALU.mult)
+            engine = nc.gpsimd if t < POOL_Y else nc.vector
+            engine.tensor_scalar(y[:, t, :], p[:, t, :], inv[:, col], 512.0, ALU.mult, ALU.mult)
             nc.sync.dma_start(out_rows[:, t, :], y[:, t, :])
 
         y_bf = sb.tile([P, SLOTS, 4], BF16, name="y_bf", align_bytes=64)

@@ -15,12 +15,14 @@ ACT = mybir.ActivationFunctionType
 AXIS = mybir.AxisListType
 
 P = 128
+PACK = 4
 D, T, SLOTS, Q = 512, 1024, 512, 512
 HALF = SLOTS // 2
+SLOT_TILES = SLOTS // P
+OUT_SCALE = 512.0
 FLOPS = 2 * D * Q * SLOTS
-V_COLS = 320
-LOADS = "c0 l3 k0 l2 l1 k1 s0 q c1 k2 k3 s1".split()
-POOL_Y = 0
+VECTOR_SLOTS = 336
+MX_ALIGN = 64
 
 
 def tile_attend_ropemerge_pl_kernel(tc, query, keys, cosn, sinn, ka, kb, offs, offs2, offs3, out_0, out_1, out_2):
@@ -29,78 +31,75 @@ def tile_attend_ropemerge_pl_kernel(tc, query, keys, cosn, sinn, ka, kb, offs, o
         sb = ctx.enter_context(tc.tile_pool(name="sb", bufs=1))
         ps = ctx.enter_context(tc.psum_pool(name="ps", bufs=1))
 
-        def plane(src, t, name):
-            tile = sb.tile([P, T], F32, name=name, tag=name)
-            nc.sync.dma_start(tile[:], src.rearrange("(p t) n -> p t n", t=4)[:, t, :])
+        def load_plane(src, t, name):
+            tile = sb.tile([P, T], F32, name=name, tag=name, align_bytes=MX_ALIGN)
+            nc.sync.dma_start(tile[:], src.rearrange("(p t) n -> p t n", t=PACK)[:, t, :])
             return tile
 
-        def offsets(src, name):
+        def load_list(src, name):
             tile = sb.tile([P, SLOTS // 16], U16, name=name)
             nc.sync.dma_start(tile[:], src)
             return tile
 
-        key = [None] * 4
-        cos = [None] * 2
-        sin = [None] * 2
+        def load_query_half(h):
+            nc.sync.dma_start(q_raw[h][:], query.rearrange("(p j) q -> p j q", j=PACK)[:, :, h * (Q // 2) : (h + 1) * (Q // 2)])
+
         share_rows = sb.tile([P, P], F32, name="share_rows")
         nc.gpsimd.memset(share_rows[:], 0.0)
-        nc.scalar.dma_start(share_rows[0:4, :], ka.rearrange("o (s i) -> (o s) i", s=4))
-        nc.scalar.dma_start(share_rows[4:8, :], kb.rearrange("o (s i) -> (o s) i", s=4))
-        q_raw = sb.tile([P, 4, Q], F32, name="q_raw")
-        for item in LOADS:
-            if item[0] == "k":
-                key[int(item[1])] = plane(keys, int(item[1]), "key" + item[1])
-            elif item[0] == "c":
-                cos[int(item[1])] = plane(cosn, 2 * int(item[1]), "cos" + item[1])
-            elif item[0] == "s":
-                sin[int(item[1])] = plane(sinn, 2 * int(item[1]), "sin" + item[1])
-            elif item == "q":
-                nc.sync.dma_start(q_raw[:], query.rearrange("(p j) q -> p j q", j=4))
-            elif item == "l1":
-                list1 = offsets(offs, "list1")
-            elif item == "l2":
-                list2 = offsets(offs2, "list2")
-            else:
-                list3 = offsets(offs3, "list3")
+        nc.scalar.dma_start(share_rows[0:SLOT_TILES, :], ka.rearrange("o (s i) -> (o s) i", s=SLOT_TILES))
+        nc.scalar.dma_start(share_rows[SLOT_TILES : 2 * SLOT_TILES, :], kb.rearrange("o (s i) -> (o s) i", s=SLOT_TILES))
+        q_raw = [sb.tile([P, PACK, Q // 2], F32, name=f"q_raw{h}") for h in range(2)]
+
+        key, cos, sin = {}, {}, {}
+        cos[0] = load_plane(cosn, 0, "cos0")
+        distance_list = load_list(offs3, "distance_list")
+        key[0] = load_plane(keys, 0, "key0")
+        second_list = load_list(offs2, "second_list")
+        first_list = load_list(offs, "first_list")
+        load_query_half(0)
+        key[1] = load_plane(keys, 1, "key1")
+        load_query_half(1)
+        sin[0] = load_plane(sinn, 0, "sin0")
+        cos[1] = load_plane(cosn, 2, "cos1")
+        key[2] = load_plane(keys, 2, "key2")
+        key[3] = load_plane(keys, 3, "key3")
+        sin[1] = load_plane(sinn, 2, "sin1")
 
         ident = sb.tile([P, P], F32, name="ident")
         make_identity(nc, ident[:])
 
-        warm = sb.tile([P, 8], F32, name="warm")
-        nc.scalar.activation(warm[:], ident[:, 0:8], ACT.Exp)
-
         def ring_bank(name):
             return ps.tile([P, 4, P], F32, name=name, tag="ring", bufs=4)
 
-        bank = ring_bank("share_bank")
-        nc.tensor.transpose(bank[:, 0, :], share_rows[:], ident[:])
-        shares = sb.tile([P, 8], F32, name="shares")
-        nc.scalar.copy(shares[:], bank[:, 0, 0:8])
-        bank = ring_bank("ka_bank")
-        for s in range(4):
-            nc.tensor.transpose(bank[:, s, :], shares[:, s : s + 1].to_broadcast([P, P]), ident[:])
+        share_bank = ring_bank("share_bank")
+        nc.tensor.transpose(share_bank[:, 0, :], share_rows[:], ident[:])
+        shares = sb.tile([P, 2 * SLOT_TILES], F32, name="shares")
+        nc.scalar.copy(shares[:], share_bank[:, 0, 0 : 2 * SLOT_TILES])
+        ka_bank = ring_bank("ka_bank")
+        for s in range(SLOT_TILES):
+            nc.tensor.transpose(ka_bank[:, s, :], shares[:, s : s + 1].to_broadcast([P, P]), ident[:])
         ka_row = sb.tile([P, SLOTS], F32, name="ka_row")
-        nc.scalar.copy(ka_row[:], bank[:].rearrange("j s i -> j (s i)"))
+        nc.scalar.copy(ka_row[:], ka_bank[:].rearrange("j s i -> j (s i)"))
 
-        def gathered(table, offs_tile, name, align=None):
-            tile = sb.tile([P, SLOTS], F32, name=name, tag=name, align_bytes=64)
-            nc.vector.tensor_copy(tile[:], table[:].indirect(offs_tile[:]))
+        def gather(table, offsets, name):
+            tile = sb.tile([P, SLOTS], F32, name=name, tag=name, align_bytes=MX_ALIGN)
+            nc.vector.tensor_copy(tile[:], table[:].indirect(offsets[:]))
             return tile
 
         def second_keys(u):
-            c = gathered(cos[u], list3, f"c{u}")
-            g = [gathered(key[2 * u + e], list2, f"g{u}{e}") for e in range(2)]
-            with_cos = sb.tile([P, 2, SLOTS], F32, name=f"pc{u}")
+            c = gather(cos[u], distance_list, f"c{u}")
+            second = [gather(key[2 * u + e], second_list, f"second{u}{e}") for e in range(2)]
+            with_cos = sb.tile([P, 2, SLOTS], F32, name=f"with_cos{u}")
             for e in range(2):
-                nc.gpsimd.tensor_tensor(with_cos[:, e, :], g[e][:], c[:], ALU.mult)
-            return g, with_cos
+                nc.gpsimd.tensor_tensor(with_cos[:, e, :], second[e][:], c[:], ALU.mult)
+            return second, with_cos
 
-        merged = [ps.tile([P, 4, P], F32, name=f"merged{s}") for s in range(4)]
+        merged = [ps.tile([P, PACK, P], F32, name=f"merged{s}") for s in range(SLOT_TILES)]
 
-        def add_share(u, lo, terms, second, opens, closes):
-            name = f"{u}_{lo}_{second}"
+        def add_share(u, lo, terms, share, opens, closes):
+            name = f"{u}_{lo}_{share}"
             bank = ring_bank("turned" + name)
-            passes = [(term, s, e) for term in terms for e in range(2) for s in range(2)]
+            passes = [(term, s, e) for term, e in terms for s in range(2)]
             for k, (term, s, e) in enumerate(passes):
                 at = lo + s * P
                 nc.tensor.matmul(
@@ -108,103 +107,128 @@ def tile_attend_ropemerge_pl_kernel(tc, query, keys, cosn, sinn, ka, kb, offs, o
                     is_transpose=True, start=(k == 0), stop=(k == len(passes) - 1),
                 )
             for s in range(2):
-                tile_no = lo // P + s
-                col = 4 * second + tile_no
+                slot_tile = lo // P + s
+                col = SLOT_TILES * share + slot_tile
                 scaled = sb.tile([P, 2, P], F32, name=f"scaled{name}_{s}")
                 nc.scalar.activation(scaled[:], bank[:, 2 * s : 2 * s + 2, :], ACT.Copy, scale=shares[:, col : col + 1])
                 for e in range(2):
                     nc.tensor.matmul(
-                        merged[tile_no][:, 2 * u + e, :], lhsT=scaled[:, e, :], rhs=ident[:], is_transpose=True,
+                        merged[slot_tile][:, 2 * u + e, :], lhsT=scaled[:, e, :], rhs=ident[:], is_transpose=True,
                         start=(opens and e == 0), stop=(closes and e == 1),
                     )
 
-        km = sb.tile([P, SLOTS, 4], BF16, name="km", align_bytes=64)
+        def rotation_terms(with_cos, with_sin):
+            return ((with_cos, 0), (with_cos, 1), (with_sin, 1), (with_sin, 0))
 
-        g, with_cos = second_keys(0)
+        km = [sb.tile([P, HALF, PACK], BF16, name=f"km{h}", tag=f"km{h}", align_bytes=MX_ALIGN) for h in range(2)]
+
+        def km_pair(s, u):
+            return km[s // 2][:, (s % 2) * P : (s % 2 + 1) * P, 2 * u : 2 * u + 2]
+
+        def merged_pair(s, u):
+            return merged[s][:, 2 * u : 2 * u + 2, :].rearrange("p e i -> p i e")
+
+        q_bf = sb.tile([P, PACK, P, PACK], BF16, name="q_bf", align_bytes=MX_ALIGN)
+        for h in range(2):
+            nc.scalar.copy(
+                q_bf[:].rearrange("p t m j -> p m j t")[:, h * (P // 2) : (h + 1) * (P // 2), :, :],
+                q_raw[h][:].rearrange("p j (m t) -> p m j t", t=PACK),
+            )
+
+        second, with_cos = second_keys(0)
         first = sb.tile([P, 2, SLOTS], F32, name="first0")
         for e in range(2):
-            nc.vector.tensor_copy(first[:, e, :], key[e][:].indirect(list1[:]))
-        s0 = gathered(sin[0], list3, "s0")
-        minus_s0 = sb.tile([P, SLOTS], F32, name="minus_s0")
-        nc.scalar.mul(minus_s0[:], s0[:], -1.0)
-        with_sin = sb.tile([P, 2, SLOTS], F32, name="ps0")
-        nc.gpsimd.tensor_tensor(with_sin[:, 1, :], g[0][:], s0[:], ALU.mult)
-        nc.gpsimd.tensor_tensor(with_sin[:, 0, :], g[1][:], minus_s0[:], ALU.mult)
+            nc.vector.tensor_copy(first[:, e, :], key[e][:].indirect(first_list[:]))
+        minus_odd = sb.tile([P, SLOTS], F32, name="minus_odd")
+        nc.gpsimd.tensor_scalar(minus_odd[:], second[1][:], -1.0, 0.0, ALU.mult, ALU.add)
+        s0 = gather(sin[0], distance_list, "s0")
+        with_sin = sb.tile([P, 2, SLOTS], F32, name="with_sin0")
+        nc.gpsimd.tensor_tensor(with_sin[:, 1, :], second[0][:], s0[:], ALU.mult)
+        nc.gpsimd.tensor_tensor(with_sin[:, 0, :], minus_odd[:], s0[:], ALU.mult)
         for lo in (0, HALF):
-            add_share(0, lo, (first,), 0, True, False)
-        q_bf = sb.tile([P, 4, P, 4], BF16, name="q_bf", align_bytes=64)
-        for m in range(0, P, 32):
-            nc.scalar.copy(
-                q_bf[:].rearrange("p t m j -> p m j t")[:, m : m + 32, :, :],
-                q_raw[:].rearrange("p j (m t) -> p m j t", t=4)[:, m : m + 32, :, :],
-            )
+            add_share(0, lo, ((first, 0), (first, 1)), 0, True, False)
         for lo in (0, HALF):
-            add_share(0, lo, (with_cos, with_sin), 1, False, True)
-        for s in range(4):
-            nc.scalar.copy(km[:, s * P : (s + 1) * P, 0:2], merged[s][:, 0:2, :].rearrange("p e i -> p i e"))
+            add_share(0, lo, rotation_terms(with_cos, with_sin), 1, False, True)
+        for s in range(SLOT_TILES):
+            nc.scalar.copy(km_pair(s, 0), merged_pair(s, 0))
 
-        g, with_cos = second_keys(1)
-        s1 = gathered(sin[1], list3, "s1")
-        with_sin = sb.tile([P, 2, SLOTS], F32, name="ps1")
+        second, with_cos = second_keys(1)
+        s1 = gather(sin[1], distance_list, "s1")
+        with_sin = sb.tile([P, 2, SLOTS], F32, name="with_sin1")
         for lo in (0, HALF):
             cols = slice(lo, lo + HALF)
-            nc.vector.tensor_tensor(with_sin[:, 1, cols], g[0][:, cols], s1[:, cols], ALU.mult)
-            nc.vector.scalar_tensor_tensor(with_sin[:, 0, cols], g[1][:, cols], -1.0, s1[:, cols], ALU.mult, ALU.mult)
-            add_share(1, lo, (with_cos, with_sin), 1, True, True)
-        first = sb.tile([P, 2, SLOTS], F32, name="first1", tag="sin1")
+            nc.vector.tensor_tensor(with_sin[:, 1, cols], second[0][:, cols], s1[:, cols], ALU.mult)
+            nc.vector.scalar_tensor_tensor(with_sin[:, 0, cols], second[1][:, cols], -1.0, s1[:, cols], ALU.mult, ALU.mult)
+            add_share(1, lo, rotation_terms(with_cos, with_sin), 1, True, True)
+        first = sb.tile([P, 2, SLOTS], F32, name="first1", tag="sin1", align_bytes=MX_ALIGN)
         for e in range(2):
-            nc.vector.tensor_tensor(first[:, e, :], key[2 + e][:].indirect(list1[:]), ka_row[:], ALU.mult)
+            nc.vector.tensor_tensor(first[:, e, :], key[2 + e][:].indirect(first_list[:]), ka_row[:], ALU.mult)
 
-        q_codes = sb.tile([P, Q], U32, name="q_codes", align_bytes=64)
-        q_scales = sb.tile([P, Q], U8, name="q_scales", tag="s1", align_bytes=64)
-        nc.vector.quantize_mx(out=q_codes[:].bitcast(FP8X4), scales=q_scales[:], in_=q_bf[:].rearrange("p t m j -> p (t m j)"))
+        q_codes = sb.tile([P, Q], U32, name="q_codes", align_bytes=MX_ALIGN)
 
-        for s in range(4):
-            cols = slice(s * P, (s + 1) * P)
-            nc.vector.tensor_tensor(
-                km[:, cols, 2:4], merged[s][:, 2:4, :].rearrange("p e i -> p i e"), first[:, :, cols].rearrange("p e i -> p i e"), ALU.add
+        def quantise_queries(t0, t1, scales):
+            nc.vector.quantize_mx(
+                out=q_codes[:, t0 * P : t1 * P].bitcast(FP8X4), scales=scales, in_=q_bf[:, t0:t1, :, :].rearrange("p t m j -> p (t m j)")
             )
-        k_codes = sb.tile([P, SLOTS], U32, name="k_codes", align_bytes=64)
-        k_scales = sb.tile([P, SLOTS], U8, name="k_scales", align_bytes=64)
-        nc.vector.quantize_mx(out=k_codes[:].bitcast(FP8X4), scales=k_scales[:], in_=km[:].rearrange("p i t -> p (i t)"))
 
-        neg_max = sb.tile([P, 4], F32, name="neg_max")
-        sums = sb.tile([P, 4], F32, name="sums")
-        inv = sb.tile([P, 4], F32, name="inv")
-        p = sb.tile([P, 4, SLOTS], F32, name="p")
-        y = sb.tile([P, 4, SLOTS], F32, name="y")
-        out_rows = out_0.rearrange("(p t) i -> p t i", t=4)
-        for t in range(4):
+        q_scales_first = sb.tile([P, P], U8, name="q_scales_first", tag="key2", align_bytes=MX_ALIGN)
+        quantise_queries(0, 1, q_scales_first[:])
+        for s in range(SLOT_TILES):
+            nc.vector.tensor_tensor(km_pair(s, 1), merged_pair(s, 1), first[:, :, s * P : (s + 1) * P].rearrange("p e i -> p i e"), ALU.add)
+        k_codes = sb.tile([P, SLOTS], U32, name="k_codes", align_bytes=MX_ALIGN)
+        k_scales = sb.tile([P, SLOTS], U8, name="k_scales", align_bytes=MX_ALIGN)
+        for h in range(2):
+            cols = slice(h * HALF, (h + 1) * HALF)
+            nc.vector.quantize_mx(out=k_codes[:, cols].bitcast(FP8X4), scales=k_scales[:, cols], in_=km[h][:].rearrange("p i t -> p (i t)"))
+        q_scales_rest = sb.tile([P, 3 * P], U8, name="q_scales_rest", tag="km1", align_bytes=MX_ALIGN)
+        quantise_queries(1, 2, q_scales_rest[:, 0:P])
+        quantise_queries(2, 4, q_scales_rest[:, P : 3 * P])
+        q_scales = [q_scales_first[:]] + [q_scales_rest[:, t * P : (t + 1) * P] for t in range(3)]
+
+        neg_max = sb.tile([P, PACK], F32, name="neg_max")
+        sums = sb.tile([P, PACK], F32, name="sums")
+        inv = sb.tile([P, PACK], F32, name="inv")
+        weights = sb.tile([P, PACK, SLOTS], F32, name="weights")
+        y = sb.tile([P, PACK, SLOTS], F32, name="y")
+        out_rows = out_0.rearrange("(p t) i -> p t i", t=PACK)
+        for t in range(PACK):
             col = slice(t, t + 1)
             rows = slice(t * P, (t + 1) * P)
             scores = ring_bank(f"scores{t}")[:].rearrange("p s i -> p (s i)")
-            nc.tensor.matmul_mx(
-                out=scores, lhsT=q_codes[:, rows].bitcast(FP8X4), lhsT_scale=q_scales[:, rows],
-                rhs=k_codes[:].bitcast(FP8X4), rhs_scale=k_scales[:], start=True, stop=True,
-            )
+            for h in range(2):
+                cols = slice(h * HALF, (h + 1) * HALF)
+                nc.tensor.matmul_mx(
+                    out=scores[:, cols], lhsT=q_codes[:, rows].bitcast(FP8X4), lhsT_scale=q_scales[t],
+                    rhs=k_codes[:, cols].bitcast(FP8X4), rhs_scale=k_scales[:, cols], start=True, stop=True,
+                )
             nc.vector.tensor_reduce(neg_max[:, col], scores, AXIS.X, ALU.max, negate=True)
-            nc.scalar.activation(p[:, t, :], scores, ACT.Exp, bias=neg_max[:, col], accum_out=sums[:, col])
-        for t in range(4):
+            nc.scalar.activation(weights[:, t, :], scores, ACT.Exp, bias=neg_max[:, col], accum_out=sums[:, col])
+        for t in range(PACK):
             col = slice(t, t + 1)
             nc.vector.reciprocal(inv[:, col], sums[:, col])
-            engine = nc.gpsimd if t < POOL_Y else nc.vector
-            engine.tensor_scalar(y[:, t, :], p[:, t, :], inv[:, col], 512.0, ALU.mult, ALU.mult)
+            width = HALF if t == PACK - 1 else SLOTS
+            for lo in range(0, SLOTS, width):
+                nc.vector.tensor_scalar(y[:, t, lo : lo + width], weights[:, t, lo : lo + width], inv[:, col], OUT_SCALE, ALU.mult, ALU.mult)
             nc.sync.dma_start(out_rows[:, t, :], y[:, t, :])
 
-        y_bf = sb.tile([P, SLOTS, 4], BF16, name="y_bf", align_bytes=64)
+        y_bf = sb.tile([P, SLOTS, PACK], BF16, name="y_bf", align_bytes=MX_ALIGN)
 
-        def woven(cols):
+        def regrouped(cols):
             return (
                 y_bf[:, cols, :].rearrange("p (c i) t -> p c t i", i=4),
                 y[:, :, cols].rearrange("p t (c i) -> p c t i", i=4),
             )
 
-        nc.vector.tensor_copy(*woven(slice(0, V_COLS)))
-        nc.scalar.copy(*woven(slice(V_COLS, SLOTS)))
-        y_codes = sb.tile([P, SLOTS], U32, name="y_codes", align_bytes=64)
-        y_scales = sb.tile([P, SLOTS], U8, name="y_scales", align_bytes=64)
-        nc.vector.quantize_mx(out=y_codes[:].bitcast(FP8X4), scales=y_scales[:], in_=y_bf[:].rearrange("p c t -> p (c t)"))
-        nc.sync.dma_start(out_1[0].rearrange("p c r -> p (c r)").bitcast(I32), y_codes[:].bitcast(I32))
+        nc.vector.tensor_copy(*regrouped(slice(0, HALF)))
+        nc.vector.tensor_copy(*regrouped(slice(HALF, VECTOR_SLOTS)))
+        nc.scalar.copy(*regrouped(slice(VECTOR_SLOTS, SLOTS)))
+        y_codes = sb.tile([P, SLOTS], U32, name="y_codes", align_bytes=MX_ALIGN)
+        y_scales = sb.tile([P, SLOTS], U8, name="y_scales", align_bytes=MX_ALIGN)
+        out_words = out_1[0].rearrange("p c r -> p (c r)").bitcast(I32)
+        for h in range(2):
+            cols = slice(h * HALF, (h + 1) * HALF)
+            nc.vector.quantize_mx(out=y_codes[:, cols].bitcast(FP8X4), scales=y_scales[:, cols], in_=y_bf[:, cols, :].rearrange("p c t -> p (c t)"))
+            nc.sync.dma_start(out_words[:, cols], y_codes[:, cols].bitcast(I32))
         for quad in range(4):
             queue = nc.scalar if quad < 2 else nc.sync
             queue.dma_start(out_2[0, 4 * quad : 4 * quad + 4, :].bitcast(I32), y_scales[32 * quad : 32 * quad + 4, :].bitcast(I32))

from contextlib import ExitStack

import concourse.mybir as mybir
from concourse.masks import make_identity

F32 = mybir.dt.float32
BF16 = mybir.dt.bfloat16
I32 = mybir.dt.int32
U32 = mybir.dt.uint32
U16 = mybir.dt.uint16
U8 = mybir.dt.uint8
FP8X4 = mybir.dt.float8_e4m3fn_x4
ALU = mybir.AluOpType
ACT = mybir.ActivationFunctionType
AXIS = mybir.AxisListType

P = 128
PACK = 4
D, T, SLOTS, Q = 512, 1024, 512, 512
HALF = SLOTS // 2
SLOT_TILES = SLOTS // P
OUT_SCALE = 512.0
FLOPS = 2 * D * Q * SLOTS
VECTOR_SLOTS = 336
MX_ALIGN = 64


def tile_attend_ropemerge_pl_kernel(tc, query, keys, cosn, sinn, ka, kb, offs, offs2, offs3, out_0, out_1, out_2):
    nc = tc.nc
    with ExitStack() as ctx:
        sb = ctx.enter_context(tc.tile_pool(name="sb", bufs=1))
        ps = ctx.enter_context(tc.psum_pool(name="ps", bufs=1))

        def load_plane(src, t, name):
            tile = sb.tile([P, T], F32, name=name, tag=name, align_bytes=MX_ALIGN)
            nc.sync.dma_start(tile[:], src.rearrange("(p t) n -> p t n", t=PACK)[:, t, :])
            return tile

        def load_list(src, name):
            tile = sb.tile([P, SLOTS // 16], U16, name=name)
            nc.sync.dma_start(tile[:], src)
            return tile

        def load_query_half(h):
            nc.sync.dma_start(q_raw[h][:], query.rearrange("(p j) q -> p j q", j=PACK)[:, :, h * (Q // 2) : (h + 1) * (Q // 2)])

        share_rows = sb.tile([P, P], F32, name="share_rows")
        nc.gpsimd.memset(share_rows[:], 0.0)
        nc.scalar.dma_start(share_rows[0:SLOT_TILES, :], ka.rearrange("o (s i) -> (o s) i", s=SLOT_TILES))
        nc.scalar.dma_start(share_rows[SLOT_TILES : 2 * SLOT_TILES, :], kb.rearrange("o (s i) -> (o s) i", s=SLOT_TILES))
        q_raw = [sb.tile([P, PACK, Q // 2], F32, name=f"q_raw{h}") for h in range(2)]

        key, cos, sin = {}, {}, {}
        cos[0] = load_plane(cosn, 0, "cos0")
        distance_list = load_list(offs3, "distance_list")
        key[0] = load_plane(keys, 0, "key0")
        second_list = load_list(offs2, "second_list")
        first_list = load_list(offs, "first_list")
        load_query_half(0)
        key[1] = load_plane(keys, 1, "key1")
        load_query_half(1)
        sin[0] = load_plane(sinn, 0, "sin0")
        cos[1] = load_plane(cosn, 2, "cos1")
        key[2] = load_plane(keys, 2, "key2")
        key[3] = load_plane(keys, 3, "key3")
        sin[1] = load_plane(sinn, 2, "sin1")

        ident = sb.tile([P, P], F32, name="ident")
        make_identity(nc, ident[:])

        def ring_bank(name):
            return ps.tile([P, 4, P], F32, name=name, tag="ring", bufs=4)

        share_bank = ring_bank("share_bank")
        nc.tensor.transpose(share_bank[:, 0, :], share_rows[:], ident[:])
        shares = sb.tile([P, 2 * SLOT_TILES], F32, name="shares")
        nc.scalar.copy(shares[:], share_bank[:, 0, 0 : 2 * SLOT_TILES])
        ka_bank = ring_bank("ka_bank")
        for s in range(SLOT_TILES):
            nc.tensor.transpose(ka_bank[:, s, :], shares[:, s : s + 1].to_broadcast([P, P]), ident[:])
        ka_row = sb.tile([P, SLOTS], F32, name="ka_row")
        nc.scalar.copy(ka_row[:], ka_bank[:].rearrange("j s i -> j (s i)"))

        def gather(table, offsets, name):
            tile = sb.tile([P, SLOTS], F32, name=name, tag=name, align_bytes=MX_ALIGN)
            nc.vector.tensor_copy(tile[:], table[:].indirect(offsets[:]))
            return tile

        def second_keys(u):
            c = gather(cos[u], distance_list, f"c{u}")
            second = [gather(key[2 * u + e], second_list, f"second{u}{e}") for e in range(2)]
            with_cos = sb.tile([P, 2, SLOTS], F32, name=f"with_cos{u}")
            for e in range(2):
                nc.gpsimd.tensor_tensor(with_cos[:, e, :], second[e][:], c[:], ALU.mult)
            return second, with_cos

        merged = [ps.tile([P, PACK, P], F32, name=f"merged{s}") for s in range(SLOT_TILES)]

        def add_share(u, lo, terms, share, opens, closes):
            name = f"{u}_{lo}_{share}"
            bank = ring_bank("turned" + name)
            passes = [(term, s, e) for term, e in terms for s in range(2)]
            for k, (term, s, e) in enumerate(passes):
                at = lo + s * P
                nc.tensor.matmul(
                    bank[:, 2 * s + e, :], lhsT=term[:, e, at : at + P], rhs=ident[:],
                    is_transpose=True, start=(k == 0), stop=(k == len(passes) - 1),
                )
            for s in range(2):
                slot_tile = lo // P + s
                col = SLOT_TILES * share + slot_tile
                scaled = sb.tile([P, 2, P], F32, name=f"scaled{name}_{s}")
                nc.scalar.activation(scaled[:], bank[:, 2 * s : 2 * s + 2, :], ACT.Copy, scale=shares[:, col : col + 1])
                for e in range(2):
                    nc.tensor.matmul(
                        merged[slot_tile][:, 2 * u + e, :], lhsT=scaled[:, e, :], rhs=ident[:], is_transpose=True,
                        start=(opens and e == 0), stop=(closes and e == 1),
                    )

        def rotation_terms(with_cos, with_sin):
            return ((with_cos, 0), (with_cos, 1), (with_sin, 1), (with_sin, 0))

        km = [sb.tile([P, HALF, PACK], BF16, name=f"km{h}", tag=f"km{h}", align_bytes=MX_ALIGN) for h in range(2)]

        def km_pair(s, u):
            return km[s // 2][:, (s % 2) * P : (s % 2 + 1) * P, 2 * u : 2 * u + 2]

        def merged_pair(s, u):
            return merged[s][:, 2 * u : 2 * u + 2, :].rearrange("p e i -> p i e")

        q_bf = sb.tile([P, PACK, P, PACK], BF16, name="q_bf", align_bytes=MX_ALIGN)
        for h in range(2):
            nc.scalar.copy(
                q_bf[:].rearrange("p t m j -> p m j t")[:, h * (P // 2) : (h + 1) * (P // 2), :, :],
                q_raw[h][:].rearrange("p j (m t) -> p m j t", t=PACK),
            )

        second, with_cos = second_keys(0)
        first = sb.tile([P, 2, SLOTS], F32, name="first0")
        for e in range(2):
            nc.vector.tensor_copy(first[:, e, :], key[e][:].indirect(first_list[:]))
        minus_odd = sb.tile([P, SLOTS], F32, name="minus_odd")
        nc.gpsimd.tensor_scalar(minus_odd[:], second[1][:], -1.0, 0.0, ALU.mult, ALU.add)
        s0 = gather(sin[0], distance_list, "s0")
        with_sin = sb.tile([P, 2, SLOTS], F32, name="with_sin0")
        nc.gpsimd.tensor_tensor(with_sin[:, 1, :], second[0][:], s0[:], ALU.mult)
        nc.gpsimd.tensor_tensor(with_sin[:, 0, :], minus_odd[:], s0[:], ALU.mult)
        for lo in (0, HALF):
            add_share(0, lo, ((first, 0), (first, 1)), 0, True, False)
        for lo in (0, HALF):
            add_share(0, lo, rotation_terms(with_cos, with_sin), 1, False, True)
        for s in range(SLOT_TILES):
            nc.scalar.copy(km_pair(s, 0), merged_pair(s, 0))

        second, with_cos = second_keys(1)
        s1 = gather(sin[1], distance_list, "s1")
        with_sin = sb.tile([P, 2, SLOTS], F32, name="with_sin1")
        for lo in (0, HALF):
            cols = slice(lo, lo + HALF)
            nc.vector.tensor_tensor(with_sin[:, 1, cols], second[0][:, cols], s1[:, cols], ALU.mult)
            nc.vector.scalar_tensor_tensor(with_sin[:, 0, cols], second[1][:, cols], -1.0, s1[:, cols], ALU.mult, ALU.mult)
            add_share(1, lo, rotation_terms(with_cos, with_sin), 1, True, True)
        first = sb.tile([P, 2, SLOTS], F32, name="first1", tag="sin1", align_bytes=MX_ALIGN)
        for e in range(2):
            nc.vector.tensor_tensor(first[:, e, :], key[2 + e][:].indirect(first_list[:]), ka_row[:], ALU.mult)

        q_codes = sb.tile([P, Q], U32, name="q_codes", align_bytes=MX_ALIGN)

        def quantise_queries(t0, t1, scales):
            nc.vector.quantize_mx(
                out=q_codes[:, t0 * P : t1 * P].bitcast(FP8X4), scales=scales, in_=q_bf[:, t0:t1, :, :].rearrange("p t m j -> p (t m j)")
            )

        q_scales_first = sb.tile([P, P], U8, name="q_scales_first", tag="key2", align_bytes=MX_ALIGN)
        quantise_queries(0, 1, q_scales_first[:])
        for s in range(SLOT_TILES):
            nc.vector.tensor_tensor(km_pair(s, 1), merged_pair(s, 1), first[:, :, s * P : (s + 1) * P].rearrange("p e i -> p i e"), ALU.add)
        k_codes = sb.tile([P, SLOTS], U32, name="k_codes", align_bytes=MX_ALIGN)
        k_scales = sb.tile([P, SLOTS], U8, name="k_scales", align_bytes=MX_ALIGN)
        for h in range(2):
            cols = slice(h * HALF, (h + 1) * HALF)
            nc.vector.quantize_mx(out=k_codes[:, cols].bitcast(FP8X4), scales=k_scales[:, cols], in_=km[h][:].rearrange("p i t -> p (i t)"))
        q_scales_rest = sb.tile([P, 3 * P], U8, name="q_scales_rest", tag="km1", align_bytes=MX_ALIGN)
        quantise_queries(1, 2, q_scales_rest[:, 0:P])
        quantise_queries(2, 4, q_scales_rest[:, P : 3 * P])
        q_scales = [q_scales_first[:]] + [q_scales_rest[:, t * P : (t + 1) * P] for t in range(3)]

        neg_max = sb.tile([P, PACK], F32, name="neg_max")
        sums = sb.tile([P, PACK], F32, name="sums")
        inv = sb.tile([P, PACK], F32, name="inv")
        weights = sb.tile([P, PACK, SLOTS], F32, name="weights")
        y = sb.tile([P, PACK, SLOTS], F32, name="y")
        out_rows = out_0.rearrange("(p t) i -> p t i", t=PACK)
        for t in range(PACK):
            col = slice(t, t + 1)
            rows = slice(t * P, (t + 1) * P)
            scores = ring_bank(f"scores{t}")[:].rearrange("p s i -> p (s i)")
            for h in range(2):
                cols = slice(h * HALF, (h + 1) * HALF)
                nc.tensor.matmul_mx(
                    out=scores[:, cols], lhsT=q_codes[:, rows].bitcast(FP8X4), lhsT_scale=q_scales[t],
                    rhs=k_codes[:, cols].bitcast(FP8X4), rhs_scale=k_scales[:, cols], start=True, stop=True,
                )
            nc.vector.tensor_reduce(neg_max[:, col], scores, AXIS.X, ALU.max, negate=True)
            nc.scalar.activation(weights[:, t, :], scores, ACT.Exp, bias=neg_max[:, col], accum_out=sums[:, col])
        for t in range(PACK):
            col = slice(t, t + 1)
            nc.vector.reciprocal(inv[:, col], sums[:, col])
            width = HALF if t == PACK - 1 else SLOTS
            for lo in range(0, SLOTS, width):
                nc.vector.tensor_scalar(y[:, t, lo : lo + width], weights[:, t, lo : lo + width], inv[:, col], OUT_SCALE, ALU.mult, ALU.mult)
            nc.sync.dma_start(out_rows[:, t, :], y[:, t, :])

        y_bf = sb.tile([P, SLOTS, PACK], BF16, name="y_bf", align_bytes=MX_ALIGN)

        def regrouped(cols):
            return (
                y_bf[:, cols, :].rearrange("p (c i) t -> p c t i", i=4),
                y[:, :, cols].rearrange("p t (c i) -> p c t i", i=4),
            )

        nc.vector.tensor_copy(*regrouped(slice(0, HALF)))
        nc.vector.tensor_copy(*regrouped(slice(HALF, VECTOR_SLOTS)))
        nc.scalar.copy(*regrouped(slice(VECTOR_SLOTS, SLOTS)))
        y_codes = sb.tile([P, SLOTS], U32, name="y_codes", align_bytes=MX_ALIGN)
        y_scales = sb.tile([P, SLOTS], U8, name="y_scales", align_bytes=MX_ALIGN)
        out_words = out_1[0].rearrange("p c r -> p (c r)").bitcast(I32)
        for h in range(2):
            cols = slice(h * HALF, (h + 1) * HALF)
            nc.vector.quantize_mx(out=y_codes[:, cols].bitcast(FP8X4), scales=y_scales[:, cols], in_=y_bf[:, cols, :].rearrange("p c t -> p (c t)"))
            nc.sync.dma_start(out_words[:, cols], y_codes[:, cols].bitcast(I32))
        for quad in range(4):
            queue = nc.scalar if quad < 2 else nc.sync
            queue.dma_start(out_2[0, 4 * quad : 4 * quad + 4, :].bitcast(I32), y_scales[32 * quad : 32 * quad + 4, :].bitcast(I32))
